import numpy as np
import ml_dtypes


def mxq(x, axis, fmt="e4m3"):
    dtype, down = {"e4m3": (ml_dtypes.float8_e4m3fn, 7), "e5m2": (ml_dtypes.float8_e5m2, 14)}[fmt]
    v = np.moveaxis(np.asarray(x, np.float32).astype(ml_dtypes.bfloat16).astype(np.float64), axis, -1)
    blocks = v.reshape(v.shape[:-1] + (-1, 32))
    amax = np.abs(blocks).max(-1, keepdims=True)
    byte = np.maximum(np.where(amax > 0, np.frexp(amax)[1] - 1 + 127, 0) - down, 1)
    scale = np.exp2(byte - 127.0)
    codes = (blocks / scale).astype(np.float32).astype(dtype).astype(np.float64)
    return np.moveaxis((codes * scale).reshape(v.shape), -1, axis)


WIDE = False


def mx_kscale(k):
    if not WIDE:
        return np.ones(k)
    levels = np.array([10, -10, 5, -5, 0])
    if k % 512:
        return np.exp2(np.random.permutation(np.resize(levels, k // 32))).repeat(32)
    a = np.empty((k // 512, 16))
    for p in range(k // 512):
        a[p, :8] = np.random.permutation(np.resize(levels, 8))
        for g in range(8):
            far = levels[np.abs(levels - a[p, g]) >= 10]
            a[p, g + 8] = far[np.random.randint(len(far))]
    return np.exp2(a.ravel()).repeat(32)


def f64(x):
    return np.asarray(x).astype(np.float64)


def striped(idx):
    return np.tile(np.asarray(idx).reshape(-1, 16).T, (8, 1)).astype(np.uint16)


def unstriped(offs):
    return offs[:16].T.reshape(-1).astype(np.int64)


E2M1 = np.array([0.0, 0.5, 1.0, 1.5, 2.0, 3.0, 4.0, 6.0, -0.0, -0.5, -1.0, -1.5, -2.0, -3.0, -4.0, -6.0])


def pack_weight(w, fmt):
    k, n = w.shape
    w = f64(np.asarray(w, np.float32).astype(ml_dtypes.bfloat16)).reshape(k // 32, 32, n)
    amax = np.abs(w).max(1)
    if fmt == "e4m3":
        byte = np.frexp(amax)[1] - 1 + 127 - 7
    else:
        mant, ex = np.frexp(amax / 6.0)
        byte = np.where(mant > 0.5, ex, ex - 1) + 127
    byte = np.clip(np.where(amax > 0, byte, 1), 1, 254)
    scaled = (w * np.exp2(127.0 - byte)[:, None, :]).reshape(k, n).astype(np.float32)
    by_word = np.ascontiguousarray(scaled.reshape(k // 512, 128, 4, n).transpose(0, 1, 3, 2))
    if fmt == "e4m3":
        words = by_word.astype(ml_dtypes.float8_e4m3fn).view(np.uint8)
    else:
        c = by_word.astype(ml_dtypes.float4_e2m1fn).view(np.uint8) & 0xF
        words = (c[..., 0::2] | (c[..., 1::2] << 4)).reshape(k // 512, 128, 2 * n)
    return np.ascontiguousarray(words), np.ascontiguousarray(byte.astype(np.uint8).reshape(k // 512, 16, n))


def unpack_weight(words, scales, fmt):
    g, _, n = scales.shape
    words = np.ascontiguousarray(words).reshape(g, 128, n, -1)
    if fmt == "e4m3":
        vals = words.view(ml_dtypes.float8_e4m3fn).astype(np.float64)
    else:
        nib = np.empty((g, 128, n, 4), np.uint8)
        nib[..., 0::2] = words & 0xF
        nib[..., 1::2] = words >> 4
        vals = E2M1[nib]
    vals = vals * np.repeat(np.exp2(scales.astype(np.float64) - 127.0), 8, axis=1)[..., None]
    return vals.transpose(0, 1, 3, 2).reshape(g * 512, n)


def bf(x):
    return np.asarray(x, np.float32).astype(ml_dtypes.bfloat16)


def planes(Y):
    r, m = Y.shape
    b = f64(bf(Y)).reshape(r // 32, 32, m)
    amax = np.abs(b).max(1)
    byte = np.clip(np.where(amax > 0, np.frexp(amax)[1] - 1 + 127 - 7, 1), 1, 254)
    codes = (b * np.exp2(127.0 - byte)[:, None, :]).reshape(r, m).astype(np.float32).astype(ml_dtypes.float8_e4m3fn).view(np.uint8)
    words = codes.reshape(r // 512, 128, 4, m).transpose(0, 1, 3, 2)
    return np.ascontiguousarray(words), np.ascontiguousarray(byte.astype(np.uint8).reshape(r // 512, 16, m))


D, E, T, I, Q = 512, 512, 2048, 512, 256


def setup_inputs():
    n = np.random.standard_normal
    idx = np.random.permutation(T)[:I]
    fd = mx_kscale(D)
    fi = mx_kscale(I)
    ti = np.ones(T)
    ti[idx] = fi
    keysp = pack_weight(n((D, T)) / fd[:, None], "e4m3")
    return {
        "query": (n((D, Q)) * 1.0 / np.sqrt(D) * fd[:, None]).astype(np.float32),
        "keys_words": keysp[0],
        "keys_scales": keysp[1],
        "floor": (np.random.uniform(0.05, 0.3, (Q, 1))).astype(np.float32),
        "reserve": (np.random.uniform(20.0, 100.0, (Q, 1))).astype(np.float32),
        "os": (np.random.uniform(4.0, 16.0, (1, I)) * fi).astype(np.float32),
        "vals": (n((E, T)) / ti).astype(np.float32),
        "offs": striped(idx),
    }


def reference(query, keys_words, keys_scales, floor, reserve, os, vals, offs):
    idx = unstriped(offs)
    keysu = unpack_weight(keys_words, keys_scales, "e4m3")
    queryq = mxq(f64(query), 0, "e4m3")
    keysidxg = keysu[:, idx]
    a = queryq.T @ keysidxg
    p = np.square(a) + f64(floor)
    z = np.sum(p, axis=1, keepdims=True) + f64(reserve)
    w = p / z
    wo1 = w * f64(os)
    wt1 = wo1.T
    vt1 = f64(vals)[:, idx].T
    vt1q = mxq(vt1, 0, "e4m3")
    wt1q = mxq(wt1, 0, "e4m3")
    o = vt1q.T @ wt1q
    words, scales = planes(o)
    return o, words, scales

@@ -1,0 +1,171 @@
+from contextlib import ExitStack
+
+import concourse.mybir as mybir
+from concourse.masks import make_identity
+
+D, E, T, I, Q = 512, 512, 2048, 512, 256
+FLOPS = 2 * Q * D * I + 2 * E * I * Q
+
+F32 = mybir.dt.float32
+BF16 = mybir.dt.bfloat16
+I32 = mybir.dt.int32
+U32 = mybir.dt.uint32
+U16 = mybir.dt.uint16
+U8 = mybir.dt.uint8
+FP8X4 = mybir.dt.float8_e4m3fn_x4
+ADD = mybir.AluOpType.add
+MULT = mybir.AluOpType.mult
+ACT = mybir.ActivationFunctionType
+
+P = 128
+PACK = 4
+QT = Q // P
+
+
+def tile_attend_squareshares_pl_kernel(tc, query, keys_words, keys_scales, floor, reserve, slot_factor, vals, offs, out_0, out_1, out_2):
+    nc = tc.nc
+    with ExitStack() as ctx:
+        sb = ctx.enter_context(tc.tile_pool(name="sb", bufs=1))
+        ps = ctx.enter_context(tc.psum_pool(name="ps", bufs=1))
+
+        q_raw = sb.tile([P, PACK, Q], F32, name="q_raw")
+        nc.sync.dma_start(q_raw[:], query.rearrange("(p j) q -> p j q", j=PACK))
+        offsets = sb.tile([P, I // 16], U16, name="offsets")
+        nc.sync.dma_start(offsets[:], offs)
+        factors = sb.tile([P, PACK], F32, name="factors")
+        nc.sync.dma_start(factors[:], slot_factor.rearrange("o (p r) -> p (o r)", r=PACK))
+
+        kscale_pool = sb.tile([P, T], U8, name="kscale_pool", align_bytes=64)
+        nc.vector.memset(kscale_pool[:, 0 : T // 2].bitcast(I32), 0)
+        nc.gpsimd.memset(kscale_pool[:, T // 2 : T].bitcast(I32), 0)
+        for g in range(4):
+            nc.sync.dma_start(kscale_pool[32 * g : 32 * g + 4, :].bitcast(I32), keys_scales[0, 4 * g : 4 * g + 4, :].bitcast(I32))
+
+        kword_pool = sb.tile([P, T], I32, name="kword_pool", align_bytes=64)
+        nc.sync.dma_start(kword_pool[:], keys_words[0].rearrange("p n t -> p (n t)").bitcast(I32))
+        row_terms = sb.tile([P, P], F32, name="row_terms")
+        nc.gpsimd.memset(row_terms[:], 0.0)
+        nc.sync.dma_start(row_terms[0:QT, :], floor.rearrange("(c p) o -> c (p o)", p=P))
+        nc.sync.dma_start(row_terms[QT : 2 * QT, :], reserve.rearrange("(c p) o -> c (p o)", p=P))
+        vals_by_place = vals.rearrange("(p t) n -> p t n", t=PACK)
+        v_pool = []
+        for t in range(PACK):
+            v_pool.append(sb.tile([P, T], F32, name=f"v_pool{t}", align_bytes=64))
+            nc.sync.dma_start(v_pool[t][:], vals_by_place[:, t, :])
+
+        ident = sb.tile([P, P], F32, name="ident")
+        make_identity(nc, ident[:])
+        terms_turned = ps.tile([P, 2, P], F32, name="v_turned1")
+        nc.tensor.transpose(terms_turned[:, 0, :], row_terms[:], ident[:])
+        terms = sb.tile([P, 2 * QT], F32, name="terms")
+        nc.scalar.copy(terms[:], terms_turned[:, 0, 0 : 2 * QT])
+        floors = terms[:, 0:QT]
+        reserves = terms[:, QT : 2 * QT]
+
+        base = sb.tile([P, QT], F32, name="base")
+        for c in range(QT):
+            nc.scalar.activation(base[:, c : c + 1], floors[:, c : c + 1], ACT.Identity, bias=reserves[:, c : c + 1], scale=float(I))
+
+        q_bf = sb.tile([P, Q * PACK], BF16, name="q_bf", align_bytes=64)
+        nc.vector.tensor_copy(q_bf[:].rearrange("p (q j) -> p q j", j=PACK), q_raw[:].rearrange("p j q -> p q j"))
+        k_scales = sb.tile([P, I], U8, name="k_scales", align_bytes=64)
+        nc.vector.tensor_copy(k_scales[:], kscale_pool[:].indirect(offsets[:]))
+        q_codes = sb.tile([P, Q], U32, name="q_codes", align_bytes=64)
+        q_scales = sb.tile([P, Q], U8, name="q_scales", align_bytes=64)
+        nc.vector.quantize_mx(out=q_codes[:].bitcast(FP8X4), scales=q_scales[:], in_=q_bf[:])
+        k_codes = sb.tile([P, I], U32, name="k_codes", align_bytes=64)
+        nc.vector.tensor_copy(k_codes[:], kword_pool[:].bitcast(U32).indirect(offsets[:]))
+
+        squares = []
+        total = sb.tile([P, QT], F32, name="total")
+        for c in range(QT):
+            cols = slice(c * P, (c + 1) * P)
+            scores = ps.tile([P, I], F32, name=f"scores{c}")
+            nc.tensor.matmul_mx(out=scores[:], lhsT=q_codes[:, cols].bitcast(FP8X4), lhsT_scale=q_scales[:, cols],
+                                rhs=k_codes[:].bitcast(FP8X4), rhs_scale=k_scales[:], start=True, stop=True)
+            squares.append(sb.tile([P, PACK, P], F32, name=f"squares{c}"))
+            nc.scalar.activation(squares[c][:], scores[:].rearrange("p (s r) -> p r s", r=PACK), ACT.Square, accum_out=total[:, c : c + 1])
+
+        v_bf = [sb.tile([P, P * PACK], BF16, name=f"v_bf{t}", align_bytes=64) for t in range(PACK)]
+        v_codes = [sb.tile([P, P], U32, name=f"v_codes{t}", align_bytes=64) for t in range(PACK)]
+        v_scales = [sb.tile([P, P], U8, name=f"v_scales{t}", align_bytes=64) for t in range(PACK)]
+
+        def gather_and_turn(t):
+            picked = sb.tile([P, I], BF16, name=f"picked{t}", align_bytes=64)
+            nc.vector.tensor_copy(picked[:], v_pool[t][:].indirect(offsets[:]))
+            pairs = picked[:].bitcast(F32)
+            v_turned = ps.tile([P, 2, P], F32, name=f"v_turned{t}", tag=("scores1", "v_turned1")[t % 2])
+            for u in range(2):
+                nc.tensor.transpose(v_turned[:, u, :], pairs[:, u : 2 * P : 2], ident[:])
+            nc.scalar.copy(v_bf[t][:].bitcast(F32).rearrange("s (p u) -> s p u", u=2), v_turned[:].rearrange("s u p -> s p u"))
+
+        def quantise_values(t):
+            nc.vector.quantize_mx(out=v_codes[t][:].bitcast(FP8X4), scales=v_scales[t][:], in_=v_bf[t][:])
+
+        gather_and_turn(0)
+
+        z = sb.tile([P, QT], F32, name="z")
+        nc.vector.tensor_tensor(z[:], total[:], base[:], ADD)
+        inv_z = sb.tile([P, QT], F32, name="inv_z")
+        nc.vector.reciprocal(inv_z[:], z[:])
+        turned = []
+        for c in range(QT):
+            shares = sb.tile([P, PACK, P], F32, name=f"shares{c}")
+            nc.vector.tensor_scalar(shares[:], squares[c][:], floors[:, c : c + 1], inv_z[:, c : c + 1], ADD, MULT)
+            turned.append(ps.tile([P, PACK, P], F32, name=f"turned{c}"))
+            for r in range(PACK):
+                nc.tensor.transpose(turned[c][:, r, :], shares[:, r, :], ident[:])
+        quantise_values(0)
+        gather_and_turn(1)
+        w_bf = sb.tile([P, Q * PACK], BF16, name="w_bf", align_bytes=64)
+        for c in range(QT):
+            nc.vector.tensor_tensor(
+                w_bf[:, c * P * PACK : (c + 1) * P * PACK].rearrange("s (q r) -> s q r", r=PACK),
+                turned[c][:].rearrange("s r q -> s q r"),
+                factors[:].unsqueeze(1).to_broadcast([P, P, PACK]),
+                MULT,
+            )
+        quantise_values(1)
+        w_codes = sb.tile([P, Q], U32, name="w_codes", align_bytes=64)
+        w_scales = sb.tile([P, Q], U8, name="w_scales", align_bytes=64)
+        nc.vector.quantize_mx(out=w_codes[:].bitcast(FP8X4), scales=w_scales[:], in_=w_bf[:])
+
+        sums = [ps.tile([P, PACK, P], F32, name=f"sums{c}") for c in range(QT)]
+        result = sb.tile([P, PACK, Q], F32, name="result")
+        out_rows = out_0.rearrange("(p t) q -> p t q", t=PACK)
+        o_bf = [sb.tile([P, P * PACK], BF16, name=f"o_bf{c}", align_bytes=64) for c in range(QT)]
+
+        def multiply(t):
+            for c in range(QT):
+                cols = slice(c * P, (c + 1) * P)
+                nc.tensor.matmul_mx(out=sums[c][:, t, :], lhsT=v_codes[t][:].bitcast(FP8X4), lhsT_scale=v_scales[t][:],
+                                    rhs=w_codes[:, cols].bitcast(FP8X4), rhs_scale=w_scales[:, cols], start=True, stop=True)
+
+        def store(places, queue):
+            for c in (1, 0):
+                nc.scalar.copy(result[:, places, c * P : (c + 1) * P], sums[c][:, places, :])
+            queue.dma_start(out_rows[:, places, :], result[:, places, :])
+
+        gather_and_turn(2)
+        multiply(0)
+        multiply(1)
+        store(slice(0, 2), nc.sync)
+        gather_and_turn(3)
+        quantise_values(2)
+        multiply(2)
+        store(slice(2, 3), nc.sync)
+        quantise_values(3)
+        multiply(3)
+        nc.vector.tensor_copy(o_bf[0][:].rearrange("p (q t) -> p q t", t=PACK), sums[0][:].rearrange("p t q -> p q t"))
+        nc.scalar.copy(o_bf[1][:].rearrange("p (q t) -> p q t", t=PACK), sums[1][:].rearrange("p t q -> p q t"))
+        store(slice(3, 4), nc.scalar)
+
+        o_codes = sb.tile([P, Q], U32, name="o_codes", align_bytes=64)
+        o_scales = sb.tile([P, Q], U8, name="o_scales", align_bytes=64)
+        for c in (1, 0):
+            cols = slice(c * P, (c + 1) * P)
+            nc.vector.quantize_mx(out=o_codes[:, cols].bitcast(FP8X4), scales=o_scales[:, cols], in_=o_bf[c][:])
+        nc.sync.dma_start(out_1[0].rearrange("p c r -> p (c r)").bitcast(I32), o_codes[:].bitcast(I32))
+        for g in range(4):
+            queue = nc.sync if g < 2 else nc.scalar
+            queue.dma_start(out_2[0, 4 * g : 4 * g + 4, :].bitcast(I32), o_scales[32 * g : 32 * g + 4, :].bitcast(I32))

@@ -32,8 +32,8 @@ def tile_attend_squareshares_pl_kernel(tc, query, keys_words, keys_scales, floor
         nc.sync.dma_start(q_raw[:], query.rearrange("(p j) q -> p j q", j=PACK))
         offsets = sb.tile([P, I // 16], U16, name="offsets")
         nc.sync.dma_start(offsets[:], offs)
-        factors = sb.tile([P, PACK], F32, name="factors")
-        nc.sync.dma_start(factors[:], slot_factor.rearrange("o (p r) -> p (o r)", r=PACK))
+        floors = sb.tile([P, QT], F32, name="floors")
+        nc.sync.dma_start(floors[:], floor.rearrange("(p c) o -> p (c o)", c=QT))
 
         kscale_pool = sb.tile([P, T], U8, name="kscale_pool", align_bytes=64)
         nc.vector.memset(kscale_pool[:, 0 : T // 2].bitcast(I32), 0)
@@ -43,10 +43,10 @@ def tile_attend_squareshares_pl_kernel(tc, query, keys_words, keys_scales, floor
 
         kword_pool = sb.tile([P, T], I32, name="kword_pool", align_bytes=64)
         nc.sync.dma_start(kword_pool[:], keys_words[0].rearrange("p n t -> p (n t)").bitcast(I32))
-        row_terms = sb.tile([P, P], F32, name="row_terms")
-        nc.gpsimd.memset(row_terms[:], 0.0)
-        nc.sync.dma_start(row_terms[0:QT, :], floor.rearrange("(c p) o -> c (p o)", p=P))
-        nc.sync.dma_start(row_terms[QT : 2 * QT, :], reserve.rearrange("(c p) o -> c (p o)", p=P))
+        factors = sb.tile([P, PACK], F32, name="factors")
+        nc.gpsimd.dma_start(factors[:], slot_factor.rearrange("o (p r) -> p (o r)", r=PACK))
+        reserves = sb.tile([P, QT], F32, name="reserves")
+        nc.sync.dma_start(reserves[:], reserve.rearrange("(p c) o -> p (c o)", c=QT))
         vals_by_place = vals.rearrange("(p t) n -> p t n", t=PACK)
         v_pool = []
         for t in range(PACK):
@@ -55,19 +55,16 @@ def tile_attend_squareshares_pl_kernel(tc, query, keys_words, keys_scales, floor
 
         ident = sb.tile([P, P], F32, name="ident")
         make_identity(nc, ident[:])
-        terms_turned = ps.tile([P, 2, P], F32, name="v_turned1")
-        nc.tensor.transpose(terms_turned[:, 0, :], row_terms[:], ident[:])
-        terms = sb.tile([P, 2 * QT], F32, name="terms")
-        nc.scalar.copy(terms[:], terms_turned[:, 0, 0 : 2 * QT])
-        floors = terms[:, 0:QT]
-        reserves = terms[:, QT : 2 * QT]
+        factor_rows = ps.tile([P, PACK, P], F32, name="factor_rows")
+        for r in range(PACK):
+            nc.tensor.transpose(factor_rows[:, r, :], factors[:, r : r + 1].to_broadcast([P, P]), ident[:])
 
         base = sb.tile([P, QT], F32, name="base")
         for c in range(QT):
             nc.scalar.activation(base[:, c : c + 1], floors[:, c : c + 1], ACT.Identity, bias=reserves[:, c : c + 1], scale=float(I))
 
         q_bf = sb.tile([P, Q * PACK], BF16, name="q_bf", align_bytes=64)
-        nc.vector.tensor_copy(q_bf[:].rearrange("p (q j) -> p q j", j=PACK), q_raw[:].rearrange("p j q -> p q j"))
+        nc.vector.tensor_copy(q_bf[:].rearrange("p (c m j) -> p c m j", c=QT, j=PACK), q_raw[:].rearrange("p j (m c) -> p c m j", c=QT))
         k_scales = sb.tile([P, I], U8, name="k_scales", align_bytes=64)
         nc.vector.tensor_copy(k_scales[:], kscale_pool[:].indirect(offsets[:]))
         q_codes = sb.tile([P, Q], U32, name="q_codes", align_bytes=64)
@@ -76,89 +73,100 @@ def tile_attend_squareshares_pl_kernel(tc, query, keys_words, keys_scales, floor
         k_codes = sb.tile([P, I], U32, name="k_codes", align_bytes=64)
         nc.vector.tensor_copy(k_codes[:], kword_pool[:].bitcast(U32).indirect(offsets[:]))
 
-        squares = []
-        total = sb.tile([P, QT], F32, name="total")
+        squares, totals = [], []
         for c in range(QT):
             cols = slice(c * P, (c + 1) * P)
             scores = ps.tile([P, I], F32, name=f"scores{c}")
             nc.tensor.matmul_mx(out=scores[:], lhsT=q_codes[:, cols].bitcast(FP8X4), lhsT_scale=q_scales[:, cols],
                                 rhs=k_codes[:].bitcast(FP8X4), rhs_scale=k_scales[:], start=True, stop=True)
-            squares.append(sb.tile([P, PACK, P], F32, name=f"squares{c}"))
-            nc.scalar.activation(squares[c][:], scores[:].rearrange("p (s r) -> p r s", r=PACK), ACT.Square, accum_out=total[:, c : c + 1])
+            squares.append(sb.tile([P, I], F32, name=f"squares{c}", align_bytes=64))
+            totals.append(sb.tile([P, 1], F32, name=f"total{c}"))
+            nc.scalar.activation(squares[c][:], scores[:], ACT.Square, accum_out=totals[c][:])
+        z = [sb.tile([P, 1], F32, name=f"z{c}") for c in range(QT)]
+        for c in range(QT):
+            nc.scalar.activation(z[c][:], totals[c][:], ACT.Identity, bias=base[:, c : c + 1])
 
-        v_bf = [sb.tile([P, P * PACK], BF16, name=f"v_bf{t}", align_bytes=64) for t in range(PACK)]
-        v_codes = [sb.tile([P, P], U32, name=f"v_codes{t}", align_bytes=64) for t in range(PACK)]
-        v_scales = [sb.tile([P, P], U8, name=f"v_scales{t}", align_bytes=64) for t in range(PACK)]
+        early_bf = sb.tile([P, (2 * P + Q) * PACK], BF16, name="early_bf", align_bytes=64)
+        v_bf = [early_bf[:, t * P * PACK : (t + 1) * P * PACK] for t in (0, 1)]
+        w_bf = early_bf[:, 2 * P * PACK :]
+        for t in (2, 3):
+            late_bf = sb.tile([P, P * PACK], BF16, name=f"v_bf{t}", align_bytes=64)
+            v_bf.append(late_bf[:])
 
-        def gather_and_turn(t):
-            picked = sb.tile([P, I], BF16, name=f"picked{t}", align_bytes=64)
+        def gather_and_turn(t, tag):
+            picked = sb.tile([P, I], BF16, name=f"picked{t}", tag=tag, align_bytes=64)
             nc.vector.tensor_copy(picked[:], v_pool[t][:].indirect(offsets[:]))
             pairs = picked[:].bitcast(F32)
-            v_turned = ps.tile([P, 2, P], F32, name=f"v_turned{t}", tag=("scores1", "v_turned1")[t % 2])
+            v_turned = ps.tile([P, 2, P], F32, name=f"v_turned{t}", tag=f"v_turned{t % 2}")
             for u in range(2):
                 nc.tensor.transpose(v_turned[:, u, :], pairs[:, u : 2 * P : 2], ident[:])
-            nc.scalar.copy(v_bf[t][:].bitcast(F32).rearrange("s (p u) -> s p u", u=2), v_turned[:].rearrange("s u p -> s p u"))
+            nc.scalar.copy(v_bf[t].bitcast(F32).rearrange("s (p u) -> s p u", u=2), v_turned[:].rearrange("s u p -> s p u"))
 
-        def quantise_values(t):
-            nc.vector.quantize_mx(out=v_codes[t][:].bitcast(FP8X4), scales=v_scales[t][:], in_=v_bf[t][:])
+        gather_and_turn(0, "picked0")
 
-        gather_and_turn(0)
-
-        z = sb.tile([P, QT], F32, name="z")
-        nc.vector.tensor_tensor(z[:], total[:], base[:], ADD)
-        inv_z = sb.tile([P, QT], F32, name="inv_z")
-        nc.vector.reciprocal(inv_z[:], z[:])
-        turned = []
+        w_turned = ps.tile([P, QT, 2, P], F32, name="w_turned")
         for c in range(QT):
-            shares = sb.tile([P, PACK, P], F32, name=f"shares{c}")
-            nc.vector.tensor_scalar(shares[:], squares[c][:], floors[:, c : c + 1], inv_z[:, c : c + 1], ADD, MULT)
-            turned.append(ps.tile([P, PACK, P], F32, name=f"turned{c}"))
-            for r in range(PACK):
-                nc.tensor.transpose(turned[c][:, r, :], shares[:, r, :], ident[:])
-        quantise_values(0)
-        gather_and_turn(1)
-        w_bf = sb.tile([P, Q * PACK], BF16, name="w_bf", align_bytes=64)
-        for c in range(QT):
-            nc.vector.tensor_tensor(
-                w_bf[:, c * P * PACK : (c + 1) * P * PACK].rearrange("s (q r) -> s q r", r=PACK),
-                turned[c][:].rearrange("s r q -> s q r"),
-                factors[:].unsqueeze(1).to_broadcast([P, P, PACK]),
-                MULT,
-            )
-        quantise_values(1)
-        w_codes = sb.tile([P, Q], U32, name="w_codes", align_bytes=64)
-        w_scales = sb.tile([P, Q], U8, name="w_scales", align_bytes=64)
-        nc.vector.quantize_mx(out=w_codes[:].bitcast(FP8X4), scales=w_scales[:], in_=w_bf[:])
+            parts = sb.tile([P, I], F32, name=f"parts{c}", tag=("v_pool0", "parts1")[c], align_bytes=64)
+            nc.vector.scalar_tensor_tensor(
+                parts[:].rearrange("q (s r) -> q s r", r=PACK), squares[c][:].rearrange("q (s r) -> q s r", r=PACK),
+                floors[:, c : c + 1], factor_rows[:].rearrange("q r s -> q s r"), ADD, MULT)
+            inv_z = sb.tile([P, 1], F32, name=f"inv_z{c}", tag=("squares0", "inv_z1")[c], align_bytes=64)
+            nc.vector.reciprocal(inv_z[:], z[c][:])
+            weights = sb.tile([P, I], BF16, name=f"weights{c}", align_bytes=64)
+            nc.scalar.activation(weights[:].rearrange("q (u s e) -> q u s e", u=2, e=2), parts[:].rearrange("q (s u e) -> q u s e", u=2, e=2), ACT.Copy, scale=inv_z[:])
+            pairs = weights[:].bitcast(F32)
+            for u in range(2):
+                nc.tensor.transpose(w_turned[:, c, u, :], pairs[:, u * P : (u + 1) * P], ident[:])
+        gather_and_turn(1, "squares1")
+        nc.scalar.copy(w_bf.bitcast(F32).rearrange("s (m c u) -> s m c u", c=QT, u=2), w_turned[:].rearrange("s c u m -> s m c u"))
+        gather_and_turn(2, "picked2")
+        early_codes = sb.tile([P, 2 * P + Q], U32, name="early_codes", tag="v_pool2", align_bytes=64)
+        early_scales = sb.tile([P, 2 * P + Q], U8, name="early_scales", align_bytes=64)
+        nc.vector.quantize_mx(out=early_codes[:].bitcast(FP8X4), scales=early_scales[:], in_=early_bf[:])
+        v_codes = {t: early_codes[:, t * P : (t + 1) * P] for t in (0, 1)}
+        v_scales = {t: early_scales[:, t * P : (t + 1) * P] for t in (0, 1)}
+        w_codes, w_scales = early_codes[:, 2 * P :], early_scales[:, 2 * P :]
 
-        sums = [ps.tile([P, PACK, P], F32, name=f"sums{c}") for c in range(QT)]
+        def quantise_values(t, tag):
+            codes = sb.tile([P, P], U32, name=f"v_codes{t}", tag=tag, align_bytes=64)
+            scales = sb.tile([P, P], U8, name=f"v_scales{t}", align_bytes=64)
+            nc.vector.quantize_mx(out=codes[:].bitcast(FP8X4), scales=scales[:], in_=v_bf[t])
+            v_codes[t], v_scales[t] = codes[:], scales[:]
+
+        LAST = PACK - 1
+        sums = [ps.tile([P, LAST, P], F32, name=f"sums{c}") for c in range(QT)]
         result = sb.tile([P, PACK, Q], F32, name="result")
         out_rows = out_0.rearrange("(p t) q -> p t q", t=PACK)
-        o_bf = [sb.tile([P, P * PACK], BF16, name=f"o_bf{c}", align_bytes=64) for c in range(QT)]
+        round_copy = (nc.vector.tensor_copy, nc.scalar.copy)
 
-        def multiply(t):
+        def multiply(t, banks):
             for c in range(QT):
                 cols = slice(c * P, (c + 1) * P)
-                nc.tensor.matmul_mx(out=sums[c][:, t, :], lhsT=v_codes[t][:].bitcast(FP8X4), lhsT_scale=v_scales[t][:],
+                nc.tensor.matmul_mx(out=banks[c], lhsT=v_codes[t].bitcast(FP8X4), lhsT_scale=v_scales[t],
                                     rhs=w_codes[:, cols].bitcast(FP8X4), rhs_scale=w_scales[:, cols], start=True, stop=True)
 
-        def store(places, queue):
+        def store(places, banks, queue):
             for c in (1, 0):
-                nc.scalar.copy(result[:, places, c * P : (c + 1) * P], sums[c][:, places, :])
+                nc.scalar.copy(result[:, places, c * P : (c + 1) * P], banks[c])
             queue.dma_start(out_rows[:, places, :], result[:, places, :])
 
-        gather_and_turn(2)
-        multiply(0)
-        multiply(1)
-        store(slice(0, 2), nc.sync)
-        gather_and_turn(3)
-        quantise_values(2)
-        multiply(2)
-        store(slice(2, 3), nc.sync)
-        quantise_values(3)
-        multiply(3)
-        nc.vector.tensor_copy(o_bf[0][:].rearrange("p (q t) -> p q t", t=PACK), sums[0][:].rearrange("p t q -> p q t"))
-        nc.scalar.copy(o_bf[1][:].rearrange("p (q t) -> p q t", t=PACK), sums[1][:].rearrange("p t q -> p q t"))
-        store(slice(3, 4), nc.scalar)
+        for t in (0, 1):
+            multiply(t, [sums[c][:, t, :] for c in range(QT)])
+        store(slice(0, 2), [sums[c][:, 0:2, :] for c in range(QT)], nc.sync)
+        gather_and_turn(3, "early_bf")
+        quantise_values(2, "v_pool3")
+        multiply(2, [sums[c][:, 2, :] for c in range(QT)])
+        quantise_values(3, "v_codes3")
+        last_sums = [ps.tile([P, P], F32, name=f"last_sums{c}", tag=f"scores{c}") for c in range(QT)]
+        multiply(3, [last_sums[c][:] for c in range(QT)])
+        o_bf = [sb.tile([P, P * PACK], BF16, name=f"o_bf{c}", tag=("v_bf3", "o_bf1")[c], align_bytes=64) for c in range(QT)]
+        o_places = [o_bf[c][:].rearrange("p (q t) -> p q t", t=PACK) for c in range(QT)]
+        for c in range(QT):
+            round_copy[c](o_places[c][:, :, 0:LAST], sums[c][:].rearrange("p t q -> p q t"))
+        for c in range(QT):
+            round_copy[c](o_places[c][:, :, LAST], last_sums[c][:])
+        store(slice(2, 3), [sums[c][:, 2:3, :] for c in range(QT)], nc.sync)
+        store(3, [last_sums[c][:] for c in range(QT)], nc.scalar)
 
         o_codes = sb.tile([P, Q], U32, name="o_codes", align_bytes=64)
         o_scales = sb.tile([P, Q], U8, name="o_scales", align_bytes=64)

from contextlib import ExitStack

import concourse.mybir as mybir
from concourse.masks import make_identity

D, E, T, I, Q = 512, 512, 2048, 512, 256
FLOPS = 2 * Q * D * I + 2 * E * I * Q

F32 = mybir.dt.float32
BF16 = mybir.dt.bfloat16
I32 = mybir.dt.int32
U32 = mybir.dt.uint32
U16 = mybir.dt.uint16
U8 = mybir.dt.uint8
FP8X4 = mybir.dt.float8_e4m3fn_x4
ADD = mybir.AluOpType.add
MULT = mybir.AluOpType.mult
ACT = mybir.ActivationFunctionType

P = 128
PACK = 4
QT = Q // P


def tile_attend_squareshares_pl_kernel(tc, query, keys_words, keys_scales, floor, reserve, slot_factor, vals, offs, out_0, out_1, out_2):
    nc = tc.nc
    with ExitStack() as ctx:
        sb = ctx.enter_context(tc.tile_pool(name="sb", bufs=1))
        ps = ctx.enter_context(tc.psum_pool(name="ps", bufs=1))

        q_raw = sb.tile([P, PACK, Q], F32, name="q_raw")
        nc.sync.dma_start(q_raw[:], query.rearrange("(p j) q -> p j q", j=PACK))
        offsets = sb.tile([P, I // 16], U16, name="offsets")
        nc.sync.dma_start(offsets[:], offs)
        floors = sb.tile([P, QT], F32, name="floors")
        nc.sync.dma_start(floors[:], floor.rearrange("(p c) o -> p (c o)", c=QT))

        kscale_pool = sb.tile([P, T], U8, name="kscale_pool", align_bytes=64)
        nc.vector.memset(kscale_pool[:, 0 : T // 2].bitcast(I32), 0)
        nc.gpsimd.memset(kscale_pool[:, T // 2 : T].bitcast(I32), 0)
        for g in range(4):
            nc.sync.dma_start(kscale_pool[32 * g : 32 * g + 4, :].bitcast(I32), keys_scales[0, 4 * g : 4 * g + 4, :].bitcast(I32))

        kword_pool = sb.tile([P, T], I32, name="kword_pool", align_bytes=64)
        nc.sync.dma_start(kword_pool[:], keys_words[0].rearrange("p n t -> p (n t)").bitcast(I32))
        factors = sb.tile([P, PACK], F32, name="factors")
        nc.gpsimd.dma_start(factors[:], slot_factor.rearrange("o (p r) -> p (o r)", r=PACK))
        reserves = sb.tile([P, QT], F32, name="reserves")
        nc.sync.dma_start(reserves[:], reserve.rearrange("(p c) o -> p (c o)", c=QT))
        vals_by_place = vals.rearrange("(p t) n -> p t n", t=PACK)
        v_pool = []
        for t in range(PACK):
            v_pool.append(sb.tile([P, T], F32, name=f"v_pool{t}", align_bytes=64))
            nc.sync.dma_start(v_pool[t][:], vals_by_place[:, t, :])

        ident = sb.tile([P, P], F32, name="ident")
        make_identity(nc, ident[:])
        factor_rows = ps.tile([P, PACK, P], F32, name="factor_rows")
        for r in range(PACK):
            nc.tensor.transpose(factor_rows[:, r, :], factors[:, r : r + 1].to_broadcast([P, P]), ident[:])

        base = sb.tile([P, QT], F32, name="base")
        for c in range(QT):
            nc.scalar.activation(base[:, c : c + 1], floors[:, c : c + 1], ACT.Identity, bias=reserves[:, c : c + 1], scale=float(I))

        q_bf = sb.tile([P, Q * PACK], BF16, name="q_bf", align_bytes=64)
        nc.vector.tensor_copy(q_bf[:].rearrange("p (c m j) -> p c m j", c=QT, j=PACK), q_raw[:].rearrange("p j (m c) -> p c m j", c=QT))
        k_scales = sb.tile([P, I], U8, name="k_scales", align_bytes=64)
        nc.vector.tensor_copy(k_scales[:], kscale_pool[:].indirect(offsets[:]))
        q_codes = sb.tile([P, Q], U32, name="q_codes", align_bytes=64)
        q_scales = sb.tile([P, Q], U8, name="q_scales", align_bytes=64)
        nc.vector.quantize_mx(out=q_codes[:].bitcast(FP8X4), scales=q_scales[:], in_=q_bf[:])
        k_codes = sb.tile([P, I], U32, name="k_codes", align_bytes=64)
        nc.vector.tensor_copy(k_codes[:], kword_pool[:].bitcast(U32).indirect(offsets[:]))

        squares, totals = [], []
        for c in range(QT):
            cols = slice(c * P, (c + 1) * P)
            scores = ps.tile([P, I], F32, name=f"scores{c}")
            nc.tensor.matmul_mx(out=scores[:], lhsT=q_codes[:, cols].bitcast(FP8X4), lhsT_scale=q_scales[:, cols],
                                rhs=k_codes[:].bitcast(FP8X4), rhs_scale=k_scales[:], start=True, stop=True)
            squares.append(sb.tile([P, I], F32, name=f"squares{c}", align_bytes=64))
            totals.append(sb.tile([P, 1], F32, name=f"total{c}"))
            nc.scalar.activation(squares[c][:], scores[:], ACT.Square, accum_out=totals[c][:])
        z = [sb.tile([P, 1], F32, name=f"z{c}") for c in range(QT)]
        for c in range(QT):
            nc.scalar.activation(z[c][:], totals[c][:], ACT.Identity, bias=base[:, c : c + 1])

        early_bf = sb.tile([P, (2 * P + Q) * PACK], BF16, name="early_bf", align_bytes=64)
        v_bf = [early_bf[:, t * P * PACK : (t + 1) * P * PACK] for t in (0, 1)]
        w_bf = early_bf[:, 2 * P * PACK :]
        for t in (2, 3):
            late_bf = sb.tile([P, P * PACK], BF16, name=f"v_bf{t}", align_bytes=64)
            v_bf.append(late_bf[:])

        def gather_and_turn(t, tag):
            picked = sb.tile([P, I], BF16, name=f"picked{t}", tag=tag, align_bytes=64)
            nc.vector.tensor_copy(picked[:], v_pool[t][:].indirect(offsets[:]))
            pairs = picked[:].bitcast(F32)
            v_turned = ps.tile([P, 2, P], F32, name=f"v_turned{t}", tag=f"v_turned{t % 2}")
            for u in range(2):
                nc.tensor.transpose(v_turned[:, u, :], pairs[:, u : 2 * P : 2], ident[:])
            nc.scalar.copy(v_bf[t].bitcast(F32).rearrange("s (p u) -> s p u", u=2), v_turned[:].rearrange("s u p -> s p u"))

        gather_and_turn(0, "picked0")

        w_turned = ps.tile([P, QT, 2, P], F32, name="w_turned")
        for c in range(QT):
            parts = sb.tile([P, I], F32, name=f"parts{c}", tag=("v_pool0", "parts1")[c], align_bytes=64)
            nc.vector.scalar_tensor_tensor(
                parts[:].rearrange("q (s r) -> q s r", r=PACK), squares[c][:].rearrange("q (s r) -> q s r", r=PACK),
                floors[:, c : c + 1], factor_rows[:].rearrange("q r s -> q s r"), ADD, MULT)
            inv_z = sb.tile([P, 1], F32, name=f"inv_z{c}", tag=("squares0", "inv_z1")[c], align_bytes=64)
            nc.vector.reciprocal(inv_z[:], z[c][:])
            weights = sb.tile([P, I], BF16, name=f"weights{c}", align_bytes=64)
            nc.scalar.activation(weights[:].rearrange("q (u s e) -> q u s e", u=2, e=2), parts[:].rearrange("q (s u e) -> q u s e", u=2, e=2), ACT.Copy, scale=inv_z[:])
            pairs = weights[:].bitcast(F32)
            for u in range(2):
                nc.tensor.transpose(w_turned[:, c, u, :], pairs[:, u * P : (u + 1) * P], ident[:])
        gather_and_turn(1, "squares1")
        nc.scalar.copy(w_bf.bitcast(F32).rearrange("s (m c u) -> s m c u", c=QT, u=2), w_turned[:].rearrange("s c u m -> s m c u"))
        gather_and_turn(2, "picked2")
        early_codes = sb.tile([P, 2 * P + Q], U32, name="early_codes", tag="v_pool2", align_bytes=64)
        early_scales = sb.tile([P, 2 * P + Q], U8, name="early_scales", align_bytes=64)
        nc.vector.quantize_mx(out=early_codes[:].bitcast(FP8X4), scales=early_scales[:], in_=early_bf[:])
        v_codes = {t: early_codes[:, t * P : (t + 1) * P] for t in (0, 1)}
        v_scales = {t: early_scales[:, t * P : (t + 1) * P] for t in (0, 1)}
        w_codes, w_scales = early_codes[:, 2 * P :], early_scales[:, 2 * P :]

        def quantise_values(t, tag):
            codes = sb.tile([P, P], U32, name=f"v_codes{t}", tag=tag, align_bytes=64)
            scales = sb.tile([P, P], U8, name=f"v_scales{t}", align_bytes=64)
            nc.vector.quantize_mx(out=codes[:].bitcast(FP8X4), scales=scales[:], in_=v_bf[t])
            v_codes[t], v_scales[t] = codes[:], scales[:]

        LAST = PACK - 1
        sums = [ps.tile([P, LAST, P], F32, name=f"sums{c}") for c in range(QT)]
        result = sb.tile([P, PACK, Q], F32, name="result")
        out_rows = out_0.rearrange("(p t) q -> p t q", t=PACK)
        round_copy = (nc.vector.tensor_copy, nc.scalar.copy)

        def multiply(t, banks):
            for c in range(QT):
                cols = slice(c * P, (c + 1) * P)
                nc.tensor.matmul_mx(out=banks[c], lhsT=v_codes[t].bitcast(FP8X4), lhsT_scale=v_scales[t],
                                    rhs=w_codes[:, cols].bitcast(FP8X4), rhs_scale=w_scales[:, cols], start=True, stop=True)

        def store(places, banks, queue):
            for c in (1, 0):
                nc.scalar.copy(result[:, places, c * P : (c + 1) * P], banks[c])
            queue.dma_start(out_rows[:, places, :], result[:, places, :])

        for t in (0, 1):
            multiply(t, [sums[c][:, t, :] for c in range(QT)])
        store(slice(0, 2), [sums[c][:, 0:2, :] for c in range(QT)], nc.sync)
        gather_and_turn(3, "early_bf")
        quantise_values(2, "v_pool3")
        multiply(2, [sums[c][:, 2, :] for c in range(QT)])
        quantise_values(3, "v_codes3")
        last_sums = [ps.tile([P, P], F32, name=f"last_sums{c}", tag=f"scores{c}") for c in range(QT)]
        multiply(3, [last_sums[c][:] for c in range(QT)])
        o_bf = [sb.tile([P, P * PACK], BF16, name=f"o_bf{c}", tag=("v_bf3", "o_bf1")[c], align_bytes=64) for c in range(QT)]
        o_places = [o_bf[c][:].rearrange("p (q t) -> p q t", t=PACK) for c in range(QT)]
        for c in range(QT):
            round_copy[c](o_places[c][:, :, 0:LAST], sums[c][:].rearrange("p t q -> p q t"))
        for c in range(QT):
            round_copy[c](o_places[c][:, :, LAST], last_sums[c][:])
        store(slice(2, 3), [sums[c][:, 2:3, :] for c in range(QT)], nc.sync)
        store(3, [last_sums[c][:] for c in range(QT)], nc.scalar)

        o_codes = sb.tile([P, Q], U32, name="o_codes", align_bytes=64)
        o_scales = sb.tile([P, Q], U8, name="o_scales", align_bytes=64)
        for c in (1, 0):
            cols = slice(c * P, (c + 1) * P)
            nc.vector.quantize_mx(out=o_codes[:, cols].bitcast(FP8X4), scales=o_scales[:, cols], in_=o_bf[c][:])
        nc.sync.dma_start(out_1[0].rearrange("p c r -> p (c r)").bitcast(I32), o_codes[:].bitcast(I32))
        for g in range(4):
            queue = nc.sync if g < 2 else nc.scalar
            queue.dma_start(out_2[0, 4 * g : 4 * g + 4, :].bitcast(I32), o_scales[32 * g : 32 * g + 4, :].bitcast(I32))
